import numpy as np
import ml_dtypes


def mxq(x, axis, fmt="e4m3"):
    dtype, down = {"e4m3": (ml_dtypes.float8_e4m3fn, 7), "e5m2": (ml_dtypes.float8_e5m2, 14)}[fmt]
    v = np.moveaxis(np.asarray(x, np.float32).astype(ml_dtypes.bfloat16).astype(np.float64), axis, -1)
    blocks = v.reshape(v.shape[:-1] + (-1, 32))
    amax = np.abs(blocks).max(-1, keepdims=True)
    byte = np.maximum(np.where(amax > 0, np.frexp(amax)[1] - 1 + 127, 0) - down, 1)
    scale = np.exp2(byte - 127.0)
    codes = (blocks / scale).astype(np.float32).astype(dtype).astype(np.float64)
    return np.moveaxis((codes * scale).reshape(v.shape), -1, axis)


WIDE = False


def mx_kscale(k):
    if not WIDE:
        return np.ones(k)
    levels = np.array([10, -10, 5, -5, 0])
    if k % 512:
        return np.exp2(np.random.permutation(np.resize(levels, k // 32))).repeat(32)
    a = np.empty((k // 512, 16))
    for p in range(k // 512):
        a[p, :8] = np.random.permutation(np.resize(levels, 8))
        for g in range(8):
            far = levels[np.abs(levels - a[p, g]) >= 10]
            a[p, g + 8] = far[np.random.randint(len(far))]
    return np.exp2(a.ravel()).repeat(32)


def f64(x):
    return np.asarray(x).astype(np.float64)


def striped(idx):
    return np.tile(idx.reshape(-1, 16).T, (8, 1)).astype(np.uint16)


def unstriped(offs):
    return offs[:16].T.reshape(-1).astype(np.int64)


def sigmoid(v):
    return 1.0 / (1.0 + np.exp(-np.maximum(v, -700.0)))


K, T, E, C, H, N = 2560, 512, 2, 256, 512, 256


def by_expert(wq, xq):
    return np.concatenate([wq[e].T @ xq[:, e * C:(e + 1) * C] for e in range(E)], axis=1)


def setup_inputs():
    n = np.random.standard_normal
    s = mx_kscale(K)[:, None]
    u = mx_kscale(H)
    return {
        "xT": (n((K, T)) * s).astype(np.float32),
        "w1": (n((E, K, H)) / np.sqrt(K) / s[None]).astype(np.float32),
        "w3": (n((E, K, H)) / np.sqrt(K) / s[None] * u[None, None, :]).astype(np.float32),
        "w2": (n((E, H, N)) / np.sqrt(H) / u[None, :, None]).astype(np.float32),
        "gate": np.tile(np.random.uniform(0.2, 1.0, E * C), (N, 1)).astype(np.float32),
        "offs": striped(np.random.permutation(T)[:E * C]),
        "dst": striped(np.random.permutation(T)[:E * C]),
    }


def reference(xT, w1, w3, w2, gate, offs, dst):
    idx = unstriped(offs)
    xq = mxq(f64(xT)[:, idx], 0, "e4m3")
    h = sigmoid(by_expert(mxq(f64(w1), 1, "e4m3"), xq))
    h = h * by_expert(mxq(f64(w3), 1, "e4m3"), xq)
    y = by_expert(mxq(f64(w2), 1, "e4m3"), mxq(h, 0, "e4m3"))
    out = np.zeros((N, T))
    out[:, unstriped(dst)] = f64(gate) * y
    return out

@@ -1,0 +1,251 @@
+from contextlib import ExitStack
+
+import concourse.mybir as mybir
+
+K, T, E, C, H, N = 2560, 512, 2, 256, 512, 256
+P = 128
+PACK = 4
+K_PASS = P * PACK
+PASSES = K // K_PASS
+FLOPS = 2 * E * C * (2 * K * H + H * N)
+
+F32 = mybir.dt.float32
+BF16 = mybir.dt.bfloat16
+U32 = mybir.dt.uint32
+U16 = mybir.dt.uint16
+U8 = mybir.dt.uint8
+FP8X4 = mybir.dt.float8_e4m3fn_x4
+SIGMOID = mybir.ActivationFunctionType.Sigmoid
+MULT = mybir.AluOpType.mult
+
+VECTOR_SHARE = 44
+VECTOR_SHARE_LAST = 84
+
+
+def tile_moe_two_glu_sigmoid_kernel(tc, xT, w1, w3, w2, gate, offs, dst, out):
+    nc = tc.nc
+    with ExitStack() as ctx:
+        lists = ctx.enter_context(tc.tile_pool(name="lists", bufs=1))
+        keep = ctx.enter_context(tc.tile_pool(name="keep", bufs=1))
+        stage = ctx.enter_context(tc.tile_pool(name="stage", bufs=8))
+        work = ctx.enter_context(tc.tile_pool(name="work", bufs=4))
+        psum = ctx.enter_context(tc.psum_pool(name="psum", bufs=1))
+
+        offs_sb = lists.tile([P, E * C // 16], U16, name="offs_sb")
+        dst_sb = lists.tile([P, E * C // 16], U16, name="dst_sb")
+
+        warm_in = keep.tile([P, 1], F32, name="warm_in")
+        warm_out = keep.tile([P, 1], F32, name="warm_out")
+        nc.vector.memset(warm_in[:], 0.0)
+        nc.scalar.activation(warm_out[:], warm_in[:], SIGMOID)
+
+        bytes_all = [keep.tile([P, T], U8, name=f"bytes_all{g}", align_bytes=64) for g in range(2)]
+        bytes_slot = [keep.tile([P, E * C], U8, name=f"bytes_slot{g}", align_bytes=64) for g in range(2)]
+        for b in bytes_all:
+            nc.gpsimd.memset(b[:], 0)
+        words_all = [keep.tile([P, T], U32, name=f"words_all{s}", align_bytes=64) for s in range(PASSES)]
+        words_slot = [keep.tile([P, E * C], U32, name=f"words_slot{s}", align_bytes=64) for s in range(PASSES)]
+        gate_sb = [keep.tile([P, 2, C], F32, name=f"gate_sb{e}") for e in range(E)]
+        placed = [keep.tile([P, T], F32, name=f"placed{q}") for q in range(N // P)]
+
+        def load(rows):
+            width = rows.shape[1]
+            raw = stage.tile([P, PACK, width], F32, name=f"raw{width}", bufs=8 if width == 512 else 2)
+            nc.sync.dma_start(raw[:], rows.rearrange("(p j) w -> p j w", j=PACK))
+            return raw
+
+        def interleave(raw, permute, share):
+            width = raw.shape[2]
+            grouped = work.tile([P, width * PACK], BF16, name=f"grouped{width}", align_bytes=64)
+            if permute:
+                to = grouped[:].rearrange("p (t m j) -> p m j t", t=4, j=PACK)
+                fro = raw[:].rearrange("p j (m t) -> p m j t", t=4)
+            else:
+                to = grouped[:].rearrange("p (c i j) -> p c j i", i=4, j=PACK)
+                fro = raw[:].rearrange("p j (c i) -> p c j i", i=4)
+            blocks = width // 4
+            cut = blocks * share // 128
+            if cut > 0:
+                nc.vector.tensor_copy(to[:, :cut], fro[:, :cut])
+            if cut < blocks:
+                nc.scalar.copy(to[:, cut:], fro[:, cut:])
+            return grouped
+
+        def quantize(grouped, codes, scales):
+            nc.vector.quantize_mx(out=codes.bitcast(FP8X4), scales=scales, in_=grouped[:])
+
+        def x_scales(s):
+            return bytes_slot[s // 4], 4 * (s % 4)
+
+        def banks(base):
+            return [psum.tile([P, 512], F32, tag=f"bank{base + t}", name=f"acc{base + t}") for t in range(4)]
+
+        def gather_words(s, e):
+            nc.vector.tensor_copy(words_slot[s][:, e * C:(e + 1) * C], words_all[s][:].indirect(offs_sb[:, e * 16:(e + 1) * 16]))
+
+        def gather_bytes(g, e):
+            nc.vector.tensor_copy(bytes_slot[g][:, e * C:(e + 1) * C], bytes_all[g][:].indirect(offs_sb[:, e * 16:(e + 1) * 16]))
+
+        def multiply(acc, codes, scales, s, e):
+            plane, k = x_scales(s)
+            cols = slice(e * C, (e + 1) * C)
+            for t in range(4):
+                m = slice(t * P, (t + 1) * P)
+                nc.tensor.matmul_mx(
+                    out=acc[t][:, :C],
+                    lhsT=codes[:, m].bitcast(FP8X4),
+                    lhsT_scale=scales[:, m],
+                    rhs=words_slot[s][:, cols].bitcast(FP8X4),
+                    rhs_scale=plane[k:P, cols],
+                    start=(s == 0),
+                    stop=(s == PASSES - 1),
+                )
+
+        chunks = []
+        for s in range(PASSES):
+            chunks.append(("x", 0, s))
+            chunks.append(("w1", 0, s))
+        for s in range(PASSES):
+            chunks.append(("w3", 0, s))
+        chunks.append(("w2", 0, 0))
+        for s in range(PASSES):
+            chunks.append(("w1", 1, s))
+        for s in range(PASSES):
+            chunks.append(("w3", 1, s))
+        chunks.append(("w2", 1, 0))
+
+        weights = {"w1": w1, "w3": w3, "w2": w2}
+        made = {}
+        acc = {}
+        sig = {}
+
+        def after(kind, e, s):
+            if kind == "x":
+                gather_words(s, 0)
+                if s == 3:
+                    gather_bytes(0, 0)
+                if s == PASSES - 1:
+                    gather_bytes(1, 0)
+                return
+            if kind == "w2":
+                return
+            if kind == "w1" and e == 0:
+                if s < PASSES - 1:
+                    return
+                acc["w1"] = banks(0)
+                for r in range(PASSES):
+                    multiply(acc["w1"], *made["w1", 0, r], r, 0)
+            else:
+                if s == 0:
+                    acc[kind] = banks(0 if kind == "w1" else 4)
+                multiply(acc[kind], *made[kind, e, s], s, e)
+            if kind == "w3" and e == 0:
+                gather_words(s, 1)
+                if s < 2:
+                    gather_bytes(s, 1)
+            if s == PASSES - 1:
+                if kind == "w1":
+                    sig[e] = keep.tile([P, 4, C], F32, name=f"sig{e}")
+                    for t in range(4):
+                        nc.scalar.activation(sig[e][:, t, :], acc["w1"][t][:, :C], SIGMOID)
+                else:
+                    hidden(e)
+
+        def parts(e):
+            return 1 if e == 0 else 2
+
+        def hidden(e):
+            n_parts = parts(e)
+            width = C // n_parts
+            made["h", e] = []
+            tiles = []
+            for u in range(n_parts):
+                cols = slice(u * width, (u + 1) * width)
+                hb = keep.tile([P, 4, width], BF16, name=f"hb{e}{u}")
+                for t in range(4):
+                    nc.vector.tensor_tensor(hb[:, t, :], acc["w3"][t][:, cols], sig[e][:, t, cols], MULT)
+                hi = keep.tile([P, width * 4], BF16, name=f"hi{e}{u}", align_bytes=64)
+                tiles.append((hb, hi))
+                if e == 1 and u == 0:
+                    g, c, sc = waiting.pop(0)[:3]
+                    quantize(g, c, sc)
+                    nc.scalar.copy(hi[:].rearrange("p (c i t) -> p c t i", i=4, t=4), hb[:].rearrange("p t (c i) -> p c t i", i=4))
+            for u in range(n_parts):
+                hb, hi = tiles[u]
+                if not (e == 1 and u == 0):
+                    nc.vector.tensor_copy(hi[:].rearrange("p (c i t) -> p c t i", i=4, t=4), hb[:].rearrange("p t (c i) -> p c t i", i=4))
+                codes = keep.tile([P, width], U32, name=f"h_codes{e}{u}", align_bytes=64)
+                scales = keep.tile([P, width], U8, name=f"h_scales{e}{u}", align_bytes=64)
+                quantize(hi, codes[:], scales[:])
+                made["h", e].append((codes, scales))
+
+        def second(e):
+            n_parts = parts(e)
+            width = C // n_parts
+            codes, scales = made["w2", e, 0]
+            for u in range(n_parts):
+                h_codes, h_scales = made["h", e][u]
+                b = (4 if e == 0 else 0) + u
+                y = psum.tile([P, 512], F32, tag=f"bank{b}", name=f"y{e}{u}")
+                for q in range(N // P):
+                    n = slice(q * P, (q + 1) * P)
+                    nc.tensor.matmul_mx(
+                        out=y[:, q * width:(q + 1) * width],
+                        lhsT=codes[:, n].bitcast(FP8X4),
+                        lhsT_scale=scales[:, n],
+                        rhs=h_codes[:].bitcast(FP8X4),
+                        rhs_scale=h_scales[:],
+                        start=True,
+                        stop=True,
+                    )
+                ysb = keep.tile([P, 2 * width], F32, name=f"ysb{e}{u}")
+                nc.scalar.copy(ysb[:], y[:, :2 * width])
+                first = e * 16 + u * (width // 16)
+                for q in range(N // P):
+                    nc.vector.tensor_tensor(placed[q][:].indirect(dst_sb[:, first:first + width // 16]), ysb[:, q * width:(q + 1) * width], gate_sb[e][:, q, u * width:(u + 1) * width], MULT)
+                    if e == E - 1 and u == n_parts - 1:
+                        nc.sync.dma_start(out[q * P:(q + 1) * P, :], placed[q][:])
+
+        def load_gate(e):
+            nc.sync.dma_start(gate_sb[e][:], gate[:, e * C:(e + 1) * C].rearrange("(q p) s -> p q s", p=P))
+
+        waiting = []
+        for i, (kind, e, s) in enumerate(chunks):
+            if kind == "x":
+                raw = load(xT[s * K_PASS:(s + 1) * K_PASS, :])
+            else:
+                raw = load(weights[kind][e, s * K_PASS:(s + 1) * K_PASS, :])
+            if i == 0:
+                nc.sync.dma_start(offs_sb[:], offs)
+            if kind == "w2" and e == 0:
+                nc.sync.dma_start(dst_sb[:], dst)
+            if kind == "w2":
+                load_gate(e)
+            share = VECTOR_SHARE
+            if e == 1 and kind == "w2":
+                share = 0
+            elif e == 1 and kind == "w3" and s == PASSES - 1:
+                share = VECTOR_SHARE_LAST
+            grouped = interleave(raw, kind in ("w1", "w3"), share)
+            if kind == "x":
+                k = 4 * (s % 4)
+                codes, scales = words_all[s][:], bytes_all[s // 4][k:P, :]
+            else:
+                width = raw.shape[2]
+                codes_t = keep.tile([P, width], U32, name=f"{kind}c{e}{s}", align_bytes=64)
+                scales_t = keep.tile([P, width], U8, name=f"{kind}s{e}{s}", align_bytes=64)
+                made[kind, e, s] = (codes_t, scales_t)
+                codes, scales = codes_t[:], scales_t[:]
+            waiting.append((grouped, codes, scales, kind, e, s))
+            if len(waiting) > 1:
+                g, c, sc, kd, ee, ss = waiting.pop(0)
+                if (kd, ee, ss) == ("w3", 1, PASSES - 1):
+                    for t in range(4):
+                        m = slice(t * P, (t + 1) * P)
+                        nc.vector.quantize_mx(out=c[:, m].bitcast(FP8X4), scales=sc[:, m], in_=g[:, t * 512:(t + 1) * 512])
+                else:
+                    quantize(g, c, sc)
+                after(kd, ee, ss)
+                if kd == "w2" and ee == 0:
+                    second(0)
+        second(1)

@@ -18,8 +18,7 @@ FP8X4 = mybir.dt.float8_e4m3fn_x4
 SIGMOID = mybir.ActivationFunctionType.Sigmoid
 MULT = mybir.AluOpType.mult
 
-VECTOR_SHARE = 44
-VECTOR_SHARE_LAST = 84
+VECTOR_SHARE = {("x", 0): 40, ("w1", 0): 40, ("w3", 0): 44, ("w2", 0): 40, ("w1", 1): 40, ("w3", 1): 64, ("w2", 1): 0}
 
 
 def tile_moe_two_glu_sigmoid_kernel(tc, xT, w1, w3, w2, gate, offs, dst, out):
@@ -49,20 +48,36 @@ def tile_moe_two_glu_sigmoid_kernel(tc, xT, w1, w3, w2, gate, offs, dst, out):
         placed = [keep.tile([P, T], F32, name=f"placed{q}") for q in range(N // P)]
 
         def load(rows):
-            width = rows.shape[1]
-            raw = stage.tile([P, PACK, width], F32, name=f"raw{width}", bufs=8 if width == 512 else 2)
-            nc.sync.dma_start(raw[:], rows.rearrange("(p j) w -> p j w", j=PACK))
-            return raw
+            count, width = rows.shape[0] // K_PASS, rows.shape[1]
+            raw = stage.tile([P, count, PACK, width], F32, name=f"raw{count}_{width}", bufs={(2, 512): 4, (1, 512): 8, (1, 256): 2}[count, width])
+            nc.sync.dma_start(raw[:], rows.rearrange("(a p j) w -> p a j w", p=P, j=PACK))
+            return [raw[:, a] for a in range(count)]
+
+        def load_halves(rows):
+            view = rows.rearrange("(p j) w -> p j w", j=PACK)
+            halves = []
+            for v in range(2):
+                half = stage.tile([P, 2, H], F32, name=f"half{v}", bufs=1)
+                nc.sync.dma_start(half[:], view[:, 2 * v:2 * v + 2, :])
+                halves.append(half)
+            return halves
+
+        def interleave_halves(halves):
+            grouped = work.tile([P, H * PACK], BF16, name="grouped512", align_bytes=64)
+            to = grouped[:].rearrange("p (t m j) -> p m j t", t=4, j=PACK)
+            nc.scalar.copy(to[:, :, 0:2], halves[0][:].rearrange("p j (m t) -> p m j t", t=4))
+            nc.vector.tensor_copy(to[:, :, 2:4], halves[1][:].rearrange("p j (m t) -> p m j t", t=4))
+            return grouped
 
         def interleave(raw, permute, share):
             width = raw.shape[2]
             grouped = work.tile([P, width * PACK], BF16, name=f"grouped{width}", align_bytes=64)
             if permute:
                 to = grouped[:].rearrange("p (t m j) -> p m j t", t=4, j=PACK)
-                fro = raw[:].rearrange("p j (m t) -> p m j t", t=4)
+                fro = raw.rearrange("p j (m t) -> p m j t", t=4)
             else:
                 to = grouped[:].rearrange("p (c i j) -> p c j i", i=4, j=PACK)
-                fro = raw[:].rearrange("p j (c i) -> p c j i", i=4)
+                fro = raw.rearrange("p j (c i) -> p c j i", i=4)
             blocks = width // 4
             cut = blocks * share // 128
             if cut > 0:
@@ -101,18 +116,13 @@ def tile_moe_two_glu_sigmoid_kernel(tc, xT, w1, w3, w2, gate, offs, dst, out):
                     stop=(s == PASSES - 1),
                 )
 
-        chunks = []
-        for s in range(PASSES):
-            chunks.append(("x", 0, s))
-            chunks.append(("w1", 0, s))
-        for s in range(PASSES):
-            chunks.append(("w3", 0, s))
-        chunks.append(("w2", 0, 0))
-        for s in range(PASSES):
-            chunks.append(("w1", 1, s))
-        for s in range(PASSES):
-            chunks.append(("w3", 1, s))
-        chunks.append(("w2", 1, 0))
+        groups = [[("x", 0, 0)], [("w1", 0, 0)]]
+        for s in range(1, PASSES):
+            groups += [[("x", 0, s)], [("w1", 0, s)]]
+        for kind, e in (("w3", 0), ("w1", 1), ("w3", 1)):
+            groups += [[(kind, e, s)] for s in range(PASSES)]
+            if kind == "w3":
+                groups.append([("w2", e, 0)])
 
         weights = {"w1": w1, "w3": w3, "w2": w2}
         made = {}
@@ -198,40 +208,47 @@ def tile_moe_two_glu_sigmoid_kernel(tc, xT, w1, w3, w2, gate, offs, dst, out):
                         start=True,
                         stop=True,
                     )
-                ysb = keep.tile([P, 2 * width], F32, name=f"ysb{e}{u}")
-                nc.scalar.copy(ysb[:], y[:, :2 * width])
+                ysb = keep.tile([P, 2, width], F32, name=f"ysb{e}{u}")
+                nc.vector.tensor_tensor(ysb[:], y[:, :2 * width].rearrange("p (q c) -> p q c", q=2), gate_sb[e][:, :, u * width:(u + 1) * width], MULT)
                 first = e * 16 + u * (width // 16)
                 for q in range(N // P):
-                    nc.vector.tensor_tensor(placed[q][:].indirect(dst_sb[:, first:first + width // 16]), ysb[:, q * width:(q + 1) * width], gate_sb[e][:, q, u * width:(u + 1) * width], MULT)
+                    nc.vector.tensor_copy(placed[q][:].indirect(dst_sb[:, first:first + width // 16]), ysb[:, q, :])
                     if e == E - 1 and u == n_parts - 1:
                         nc.sync.dma_start(out[q * P:(q + 1) * P, :], placed[q][:])
 
         def load_gate(e):
             nc.sync.dma_start(gate_sb[e][:], gate[:, e * C:(e + 1) * C].rearrange("(q p) s -> p q s", p=P))
 
+        raws = {}
         waiting = []
-        for i, (kind, e, s) in enumerate(chunks):
-            if kind == "x":
-                raw = load(xT[s * K_PASS:(s + 1) * K_PASS, :])
+
+        def load_group(i, group):
+            kind, e, s = group[0]
+            source = xT if kind == "x" else weights[kind][e]
+            rows = source[s * K_PASS:(s + len(group)) * K_PASS, :]
+            if group == [("w3", 1, PASSES - 1)]:
+                raws[group[0]] = load_halves(rows)
             else:
-                raw = load(weights[kind][e, s * K_PASS:(s + 1) * K_PASS, :])
+                for key, raw in zip(group, load(rows)):
+                    raws[key] = raw
             if i == 0:
                 nc.sync.dma_start(offs_sb[:], offs)
-            if kind == "w2" and e == 0:
-                nc.sync.dma_start(dst_sb[:], dst)
             if kind == "w2":
+                if e == 0:
+                    nc.sync.dma_start(dst_sb[:], dst)
                 load_gate(e)
-            share = VECTOR_SHARE
-            if e == 1 and kind == "w2":
-                share = 0
-            elif e == 1 and kind == "w3" and s == PASSES - 1:
-                share = VECTOR_SHARE_LAST
-            grouped = interleave(raw, kind in ("w1", "w3"), share)
+
+        def process(kind, e, s):
+            raw = raws[kind, e, s]
+            if (kind, e, s) == ("w3", 1, PASSES - 1):
+                grouped = interleave_halves(raw)
+            else:
+                grouped = interleave(raw, kind in ("w1", "w3"), VECTOR_SHARE[kind, e])
             if kind == "x":
                 k = 4 * (s % 4)
                 codes, scales = words_all[s][:], bytes_all[s // 4][k:P, :]
             else:
-                width = raw.shape[2]
+                width = N if kind == "w2" else H
                 codes_t = keep.tile([P, width], U32, name=f"{kind}c{e}{s}", align_bytes=64)
                 scales_t = keep.tile([P, width], U8, name=f"{kind}s{e}{s}", align_bytes=64)
                 made[kind, e, s] = (codes_t, scales_t)
@@ -248,4 +265,9 @@ def tile_moe_two_glu_sigmoid_kernel(tc, xT, w1, w3, w2, gate, offs, dst, out):
                 after(kd, ee, ss)
                 if kd == "w2" and ee == 0:
                     second(0)
+
+        for i, group in enumerate(groups):
+            load_group(i, group)
+            for key in group:
+                process(*key)
         second(1)

@@ -18,7 +18,7 @@ FP8X4 = mybir.dt.float8_e4m3fn_x4
 SIGMOID = mybir.ActivationFunctionType.Sigmoid
 MULT = mybir.AluOpType.mult
 
-VECTOR_SHARE = {("x", 0): 40, ("w1", 0): 40, ("w3", 0): 44, ("w2", 0): 40, ("w1", 1): 40, ("w3", 1): 64, ("w2", 1): 0}
+VECTOR_SHARE = {("x", 0): 60, ("w1", 0): 60, ("w3", 0): 52, ("w2", 0): 40, ("w1", 1): 60, ("w3", 1): 72, ("w2", 1): 0}
 
 
 def tile_moe_two_glu_sigmoid_kernel(tc, xT, w1, w3, w2, gate, offs, dst, out):
@@ -168,25 +168,23 @@ def tile_moe_two_glu_sigmoid_kernel(tc, xT, w1, w3, w2, gate, offs, dst, out):
             n_parts = parts(e)
             width = C // n_parts
             made["h", e] = []
-            tiles = []
+            hb = keep.tile([P, 4, C], BF16, name=f"hb{e}")
+            for t in range(4):
+                nc.vector.tensor_tensor(hb[:, t, :], acc["w3"][t][:, :C], sig[e][:, t, :], MULT)
+            his = []
             for u in range(n_parts):
                 cols = slice(u * width, (u + 1) * width)
-                hb = keep.tile([P, 4, width], BF16, name=f"hb{e}{u}")
-                for t in range(4):
-                    nc.vector.tensor_tensor(hb[:, t, :], acc["w3"][t][:, cols], sig[e][:, t, cols], MULT)
                 hi = keep.tile([P, width * 4], BF16, name=f"hi{e}{u}", align_bytes=64)
-                tiles.append((hb, hi))
-                if e == 1 and u == 0:
-                    g, c, sc = waiting.pop(0)[:3]
-                    quantize(g, c, sc)
-                    nc.scalar.copy(hi[:].rearrange("p (c i t) -> p c t i", i=4, t=4), hb[:].rearrange("p t (c i) -> p c t i", i=4))
+                copy = nc.vector.tensor_copy if e == 1 and u == 0 else nc.scalar.copy
+                copy(hi[:].rearrange("p (c i t) -> p c t i", i=4, t=4), hb[:, :, cols].rearrange("p t (c i) -> p c t i", i=4))
+                his.append(hi)
+            if e == 1:
+                g, c, sc = waiting.pop(0)[:3]
+                quantize(g, c, sc)
             for u in range(n_parts):
-                hb, hi = tiles[u]
-                if not (e == 1 and u == 0):
-                    nc.vector.tensor_copy(hi[:].rearrange("p (c i t) -> p c t i", i=4, t=4), hb[:].rearrange("p t (c i) -> p c t i", i=4))
                 codes = keep.tile([P, width], U32, name=f"h_codes{e}{u}", align_bytes=64)
                 scales = keep.tile([P, width], U8, name=f"h_scales{e}{u}", align_bytes=64)
-                quantize(hi, codes[:], scales[:])
+                quantize(his[u], codes[:], scales[:])
                 made["h", e].append((codes, scales))
 
         def second(e):
@@ -209,10 +207,10 @@ def tile_moe_two_glu_sigmoid_kernel(tc, xT, w1, w3, w2, gate, offs, dst, out):
                         stop=True,
                     )
                 ysb = keep.tile([P, 2, width], F32, name=f"ysb{e}{u}")
-                nc.vector.tensor_tensor(ysb[:], y[:, :2 * width].rearrange("p (q c) -> p q c", q=2), gate_sb[e][:, :, u * width:(u + 1) * width], MULT)
+                nc.scalar.copy(ysb[:], y[:, :2 * width].rearrange("p (q c) -> p q c", q=2))
                 first = e * 16 + u * (width // 16)
                 for q in range(N // P):
-                    nc.vector.tensor_copy(placed[q][:].indirect(dst_sb[:, first:first + width // 16]), ysb[:, q, :])
+                    nc.vector.tensor_tensor(placed[q][:].indirect(dst_sb[:, first:first + width // 16]), ysb[:, q, :], gate_sb[e][:, q, u * width:(u + 1) * width], MULT)
                     if e == E - 1 and u == n_parts - 1:
                         nc.sync.dma_start(out[q * P:(q + 1) * P, :], placed[q][:])
 

@@ -18,7 +18,7 @@ FP8X4 = mybir.dt.float8_e4m3fn_x4
 SIGMOID = mybir.ActivationFunctionType.Sigmoid
 MULT = mybir.AluOpType.mult
 
-VECTOR_SHARE = {("x", 0): 60, ("w1", 0): 60, ("w3", 0): 52, ("w2", 0): 40, ("w1", 1): 60, ("w3", 1): 72, ("w2", 1): 0}
+VECTOR_SHARE = {("x", 0): 40, ("w1", 0): 40, ("w3", 0): 44, ("w2", 0): 40, ("w1", 1): 40, ("w3", 1): 64, ("w2", 1): 0}
 
 
 def tile_moe_two_glu_sigmoid_kernel(tc, xT, w1, w3, w2, gate, offs, dst, out):
@@ -64,22 +64,23 @@ def tile_moe_two_glu_sigmoid_kernel(tc, xT, w1, w3, w2, gate, offs, dst, out):
 
         def interleave_halves(halves):
             grouped = work.tile([P, H * PACK], BF16, name="grouped512", align_bytes=64)
-            to = grouped[:].rearrange("p (t m j) -> p m j t", t=4, j=PACK)
-            nc.scalar.copy(to[:, :, 0:2], halves[0][:].rearrange("p j (m t) -> p m j t", t=4))
-            nc.vector.tensor_copy(to[:, :, 2:4], halves[1][:].rearrange("p j (m t) -> p m j t", t=4))
+            to = grouped[:].rearrange("p (t m i j) -> p m j t i", t=4, i=2, j=PACK)
+            fro = [half[:].rearrange("p j (m i t) -> p m j t i", t=4, i=2) for half in halves]
+            nc.scalar.copy(to[:, :, 0:2], fro[0])
+            nc.vector.tensor_copy(to[:, :, 2:4], fro[1])
             return grouped
 
         def interleave(raw, permute, share):
             width = raw.shape[2]
             grouped = work.tile([P, width * PACK], BF16, name=f"grouped{width}", align_bytes=64)
             if permute:
-                to = grouped[:].rearrange("p (t m j) -> p m j t", t=4, j=PACK)
-                fro = raw.rearrange("p j (m t) -> p m j t", t=4)
+                to = grouped[:].rearrange("p (t m i j) -> p m j t i", t=4, i=2, j=PACK)
+                fro = raw.rearrange("p j (m i t) -> p m j t i", t=4, i=2)
             else:
                 to = grouped[:].rearrange("p (c i j) -> p c j i", i=4, j=PACK)
                 fro = raw.rearrange("p j (c i) -> p c j i", i=4)
-            blocks = width // 4
-            cut = blocks * share // 128
+            blocks = to.shape[1]
+            cut = blocks * share // 256 * 2
             if cut > 0:
                 nc.vector.tensor_copy(to[:, :cut], fro[:, :cut])
             if cut < blocks:
@@ -168,23 +169,25 @@ def tile_moe_two_glu_sigmoid_kernel(tc, xT, w1, w3, w2, gate, offs, dst, out):
             n_parts = parts(e)
             width = C // n_parts
             made["h", e] = []
-            hb = keep.tile([P, 4, C], BF16, name=f"hb{e}")
-            for t in range(4):
-                nc.vector.tensor_tensor(hb[:, t, :], acc["w3"][t][:, :C], sig[e][:, t, :], MULT)
-            his = []
+            tiles = []
             for u in range(n_parts):
                 cols = slice(u * width, (u + 1) * width)
+                hb = keep.tile([P, 4, width], BF16, name=f"hb{e}{u}")
+                for t in range(4):
+                    nc.vector.tensor_tensor(hb[:, t, :], acc["w3"][t][:, cols], sig[e][:, t, cols], MULT)
                 hi = keep.tile([P, width * 4], BF16, name=f"hi{e}{u}", align_bytes=64)
-                copy = nc.vector.tensor_copy if e == 1 and u == 0 else nc.scalar.copy
-                copy(hi[:].rearrange("p (c i t) -> p c t i", i=4, t=4), hb[:, :, cols].rearrange("p t (c i) -> p c t i", i=4))
-                his.append(hi)
-            if e == 1:
-                g, c, sc = waiting.pop(0)[:3]
-                quantize(g, c, sc)
+                tiles.append((hb, hi))
+                if e == 1 and u == 0:
+                    g, c, sc = waiting.pop(0)[:3]
+                    quantize(g, c, sc)
+                    nc.scalar.copy(hi[:].rearrange("p (c i t) -> p c t i", i=4, t=4), hb[:].rearrange("p t (c i) -> p c t i", i=4))
             for u in range(n_parts):
+                hb, hi = tiles[u]
+                if not (e == 1 and u == 0):
+                    nc.vector.tensor_copy(hi[:].rearrange("p (c i t) -> p c t i", i=4, t=4), hb[:].rearrange("p t (c i) -> p c t i", i=4))
                 codes = keep.tile([P, width], U32, name=f"h_codes{e}{u}", align_bytes=64)
                 scales = keep.tile([P, width], U8, name=f"h_scales{e}{u}", align_bytes=64)
-                quantize(his[u], codes[:], scales[:])
+                quantize(hi, codes[:], scales[:])
                 made["h", e].append((codes, scales))
 
         def second(e):

from contextlib import ExitStack

import concourse.mybir as mybir

K, T, E, C, H, N = 2560, 512, 2, 256, 512, 256
P = 128
PACK = 4
K_PASS = P * PACK
PASSES = K // K_PASS
FLOPS = 2 * E * C * (2 * K * H + H * N)

F32 = mybir.dt.float32
BF16 = mybir.dt.bfloat16
U32 = mybir.dt.uint32
U16 = mybir.dt.uint16
U8 = mybir.dt.uint8
FP8X4 = mybir.dt.float8_e4m3fn_x4
SIGMOID = mybir.ActivationFunctionType.Sigmoid
MULT = mybir.AluOpType.mult

VECTOR_SHARE = {("x", 0): 40, ("w1", 0): 40, ("w3", 0): 44, ("w2", 0): 40, ("w1", 1): 40, ("w3", 1): 64, ("w2", 1): 0}


def tile_moe_two_glu_sigmoid_kernel(tc, xT, w1, w3, w2, gate, offs, dst, out):
    nc = tc.nc
    with ExitStack() as ctx:
        lists = ctx.enter_context(tc.tile_pool(name="lists", bufs=1))
        keep = ctx.enter_context(tc.tile_pool(name="keep", bufs=1))
        stage = ctx.enter_context(tc.tile_pool(name="stage", bufs=8))
        work = ctx.enter_context(tc.tile_pool(name="work", bufs=4))
        psum = ctx.enter_context(tc.psum_pool(name="psum", bufs=1))

        offs_sb = lists.tile([P, E * C // 16], U16, name="offs_sb")
        dst_sb = lists.tile([P, E * C // 16], U16, name="dst_sb")

        warm_in = keep.tile([P, 1], F32, name="warm_in")
        warm_out = keep.tile([P, 1], F32, name="warm_out")
        nc.vector.memset(warm_in[:], 0.0)
        nc.scalar.activation(warm_out[:], warm_in[:], SIGMOID)

        bytes_all = [keep.tile([P, T], U8, name=f"bytes_all{g}", align_bytes=64) for g in range(2)]
        bytes_slot = [keep.tile([P, E * C], U8, name=f"bytes_slot{g}", align_bytes=64) for g in range(2)]
        for b in bytes_all:
            nc.gpsimd.memset(b[:], 0)
        words_all = [keep.tile([P, T], U32, name=f"words_all{s}", align_bytes=64) for s in range(PASSES)]
        words_slot = [keep.tile([P, E * C], U32, name=f"words_slot{s}", align_bytes=64) for s in range(PASSES)]
        gate_sb = [keep.tile([P, 2, C], F32, name=f"gate_sb{e}") for e in range(E)]
        placed = [keep.tile([P, T], F32, name=f"placed{q}") for q in range(N // P)]

        def load(rows):
            count, width = rows.shape[0] // K_PASS, rows.shape[1]
            raw = stage.tile([P, count, PACK, width], F32, name=f"raw{count}_{width}", bufs={(2, 512): 4, (1, 512): 8, (1, 256): 2}[count, width])
            nc.sync.dma_start(raw[:], rows.rearrange("(a p j) w -> p a j w", p=P, j=PACK))
            return [raw[:, a] for a in range(count)]

        def load_halves(rows):
            view = rows.rearrange("(p j) w -> p j w", j=PACK)
            halves = []
            for v in range(2):
                half = stage.tile([P, 2, H], F32, name=f"half{v}", bufs=1)
                nc.sync.dma_start(half[:], view[:, 2 * v:2 * v + 2, :])
                halves.append(half)
            return halves

        def interleave_halves(halves):
            grouped = work.tile([P, H * PACK], BF16, name="grouped512", align_bytes=64)
            to = grouped[:].rearrange("p (t m i j) -> p m j t i", t=4, i=2, j=PACK)
            fro = [half[:].rearrange("p j (m i t) -> p m j t i", t=4, i=2) for half in halves]
            nc.scalar.copy(to[:, :, 0:2], fro[0])
            nc.vector.tensor_copy(to[:, :, 2:4], fro[1])
            return grouped

        def interleave(raw, permute, share):
            width = raw.shape[2]
            grouped = work.tile([P, width * PACK], BF16, name=f"grouped{width}", align_bytes=64)
            if permute:
                to = grouped[:].rearrange("p (t m i j) -> p m j t i", t=4, i=2, j=PACK)
                fro = raw.rearrange("p j (m i t) -> p m j t i", t=4, i=2)
            else:
                to = grouped[:].rearrange("p (c i j) -> p c j i", i=4, j=PACK)
                fro = raw.rearrange("p j (c i) -> p c j i", i=4)
            blocks = to.shape[1]
            cut = blocks * share // 256 * 2
            if cut > 0:
                nc.vector.tensor_copy(to[:, :cut], fro[:, :cut])
            if cut < blocks:
                nc.scalar.copy(to[:, cut:], fro[:, cut:])
            return grouped

        def quantize(grouped, codes, scales):
            nc.vector.quantize_mx(out=codes.bitcast(FP8X4), scales=scales, in_=grouped[:])

        def x_scales(s):
            return bytes_slot[s // 4], 4 * (s % 4)

        def banks(base):
            return [psum.tile([P, 512], F32, tag=f"bank{base + t}", name=f"acc{base + t}") for t in range(4)]

        def gather_words(s, e):
            nc.vector.tensor_copy(words_slot[s][:, e * C:(e + 1) * C], words_all[s][:].indirect(offs_sb[:, e * 16:(e + 1) * 16]))

        def gather_bytes(g, e):
            nc.vector.tensor_copy(bytes_slot[g][:, e * C:(e + 1) * C], bytes_all[g][:].indirect(offs_sb[:, e * 16:(e + 1) * 16]))

        def multiply(acc, codes, scales, s, e):
            plane, k = x_scales(s)
            cols = slice(e * C, (e + 1) * C)
            for t in range(4):
                m = slice(t * P, (t + 1) * P)
                nc.tensor.matmul_mx(
                    out=acc[t][:, :C],
                    lhsT=codes[:, m].bitcast(FP8X4),
                    lhsT_scale=scales[:, m],
                    rhs=words_slot[s][:, cols].bitcast(FP8X4),
                    rhs_scale=plane[k:P, cols],
                    start=(s == 0),
                    stop=(s == PASSES - 1),
                )

        groups = [[("x", 0, 0)], [("w1", 0, 0)]]
        for s in range(1, PASSES):
            groups += [[("x", 0, s)], [("w1", 0, s)]]
        for kind, e in (("w3", 0), ("w1", 1), ("w3", 1)):
            groups += [[(kind, e, s)] for s in range(PASSES)]
            if kind == "w3":
                groups.append([("w2", e, 0)])

        weights = {"w1": w1, "w3": w3, "w2": w2}
        made = {}
        acc = {}
        sig = {}

        def after(kind, e, s):
            if kind == "x":
                gather_words(s, 0)
                if s == 3:
                    gather_bytes(0, 0)
                if s == PASSES - 1:
                    gather_bytes(1, 0)
                return
            if kind == "w2":
                return
            if kind == "w1" and e == 0:
                if s < PASSES - 1:
                    return
                acc["w1"] = banks(0)
                for r in range(PASSES):
                    multiply(acc["w1"], *made["w1", 0, r], r, 0)
            else:
                if s == 0:
                    acc[kind] = banks(0 if kind == "w1" else 4)
                multiply(acc[kind], *made[kind, e, s], s, e)
            if kind == "w3" and e == 0:
                gather_words(s, 1)
                if s < 2:
                    gather_bytes(s, 1)
            if s == PASSES - 1:
                if kind == "w1":
                    sig[e] = keep.tile([P, 4, C], F32, name=f"sig{e}")
                    for t in range(4):
                        nc.scalar.activation(sig[e][:, t, :], acc["w1"][t][:, :C], SIGMOID)
                else:
                    hidden(e)

        def parts(e):
            return 1 if e == 0 else 2

        def hidden(e):
            n_parts = parts(e)
            width = C // n_parts
            made["h", e] = []
            tiles = []
            for u in range(n_parts):
                cols = slice(u * width, (u + 1) * width)
                hb = keep.tile([P, 4, width], BF16, name=f"hb{e}{u}")
                for t in range(4):
                    nc.vector.tensor_tensor(hb[:, t, :], acc["w3"][t][:, cols], sig[e][:, t, cols], MULT)
                hi = keep.tile([P, width * 4], BF16, name=f"hi{e}{u}", align_bytes=64)
                tiles.append((hb, hi))
                if e == 1 and u == 0:
                    g, c, sc = waiting.pop(0)[:3]
                    quantize(g, c, sc)
                    nc.scalar.copy(hi[:].rearrange("p (c i t) -> p c t i", i=4, t=4), hb[:].rearrange("p t (c i) -> p c t i", i=4))
            for u in range(n_parts):
                hb, hi = tiles[u]
                if not (e == 1 and u == 0):
                    nc.vector.tensor_copy(hi[:].rearrange("p (c i t) -> p c t i", i=4, t=4), hb[:].rearrange("p t (c i) -> p c t i", i=4))
                codes = keep.tile([P, width], U32, name=f"h_codes{e}{u}", align_bytes=64)
                scales = keep.tile([P, width], U8, name=f"h_scales{e}{u}", align_bytes=64)
                quantize(hi, codes[:], scales[:])
                made["h", e].append((codes, scales))

        def second(e):
            n_parts = parts(e)
            width = C // n_parts
            codes, scales = made["w2", e, 0]
            for u in range(n_parts):
                h_codes, h_scales = made["h", e][u]
                b = (4 if e == 0 else 0) + u
                y = psum.tile([P, 512], F32, tag=f"bank{b}", name=f"y{e}{u}")
                for q in range(N // P):
                    n = slice(q * P, (q + 1) * P)
                    nc.tensor.matmul_mx(
                        out=y[:, q * width:(q + 1) * width],
                        lhsT=codes[:, n].bitcast(FP8X4),
                        lhsT_scale=scales[:, n],
                        rhs=h_codes[:].bitcast(FP8X4),
                        rhs_scale=h_scales[:],
                        start=True,
                        stop=True,
                    )
                ysb = keep.tile([P, 2, width], F32, name=f"ysb{e}{u}")
                nc.scalar.copy(ysb[:], y[:, :2 * width].rearrange("p (q c) -> p q c", q=2))
                first = e * 16 + u * (width // 16)
                for q in range(N // P):
                    nc.vector.tensor_tensor(placed[q][:].indirect(dst_sb[:, first:first + width // 16]), ysb[:, q, :], gate_sb[e][:, q, u * width:(u + 1) * width], MULT)
                    if e == E - 1 and u == n_parts - 1:
                        nc.sync.dma_start(out[q * P:(q + 1) * P, :], placed[q][:])

        def load_gate(e):
            nc.sync.dma_start(gate_sb[e][:], gate[:, e * C:(e + 1) * C].rearrange("(q p) s -> p q s", p=P))

        raws = {}
        waiting = []

        def load_group(i, group):
            kind, e, s = group[0]
            source = xT if kind == "x" else weights[kind][e]
            rows = source[s * K_PASS:(s + len(group)) * K_PASS, :]
            if group == [("w3", 1, PASSES - 1)]:
                raws[group[0]] = load_halves(rows)
            else:
                for key, raw in zip(group, load(rows)):
                    raws[key] = raw
            if i == 0:
                nc.sync.dma_start(offs_sb[:], offs)
            if kind == "w2":
                if e == 0:
                    nc.sync.dma_start(dst_sb[:], dst)
                load_gate(e)

        def process(kind, e, s):
            raw = raws[kind, e, s]
            if (kind, e, s) == ("w3", 1, PASSES - 1):
                grouped = interleave_halves(raw)
            else:
                grouped = interleave(raw, kind in ("w1", "w3"), VECTOR_SHARE[kind, e])
            if kind == "x":
                k = 4 * (s % 4)
                codes, scales = words_all[s][:], bytes_all[s // 4][k:P, :]
            else:
                width = N if kind == "w2" else H
                codes_t = keep.tile([P, width], U32, name=f"{kind}c{e}{s}", align_bytes=64)
                scales_t = keep.tile([P, width], U8, name=f"{kind}s{e}{s}", align_bytes=64)
                made[kind, e, s] = (codes_t, scales_t)
                codes, scales = codes_t[:], scales_t[:]
            waiting.append((grouped, codes, scales, kind, e, s))
            if len(waiting) > 1:
                g, c, sc, kd, ee, ss = waiting.pop(0)
                if (kd, ee, ss) == ("w3", 1, PASSES - 1):
                    for t in range(4):
                        m = slice(t * P, (t + 1) * P)
                        nc.vector.quantize_mx(out=c[:, m].bitcast(FP8X4), scales=sc[:, m], in_=g[:, t * 512:(t + 1) * 512])
                else:
                    quantize(g, c, sc)
                after(kd, ee, ss)
                if kd == "w2" and ee == 0:
                    second(0)

        for i, group in enumerate(groups):
            load_group(i, group)
            for key in group:
                process(*key)
        second(1)
